import numpy as np, ml_dtypes
CORES = [66,70,74,78,82,86,90,94,98,102,106,110,114,118,122,126]
N = 16
TK = 128
def silu(z): return z / (1.0 + np.exp(-z))
def setup_inputs(rng):
    return {"x": rng.standard_normal((N, 128, TK), dtype=np.float32).astype(ml_dtypes.bfloat16), "w1": (rng.standard_normal((N, 128, 128), dtype=np.float32) / 8).astype(ml_dtypes.bfloat16), "w3": (rng.standard_normal((N, 128, 128), dtype=np.float32) / 8).astype(ml_dtypes.bfloat16), "w2": (rng.standard_normal((N, 128, 128), dtype=np.float32) / 8).astype(ml_dtypes.bfloat16)}
def setup_inputs_big(rng):
    d = setup_inputs(rng)
    for k in ("x",): d[k] = (d[k].astype(np.float32) * 1024.0).astype(d[k].dtype)
    return d
def setup_inputs_small(rng):
    d = setup_inputs(rng)
    for k in ("x",): d[k] = (d[k].astype(np.float32) * (1 / 1024.0)).astype(d[k].dtype)
    return d
def setup_inputs_apart(rng):
    d = setup_inputs(rng)
    f = (10.0 ** rng.permutation(np.linspace(-1.5, 1.5, N))).astype(np.float32).reshape(N, 1, 1)
    for k in ("x",): d[k] = (d[k].astype(np.float32) * f).astype(d[k].dtype)
    return d
def reference(x, w1, w3, w2):
    X, W1, W3, W2 = x.astype(np.float64), w1.astype(np.float64), w3.astype(np.float64), w2.astype(np.float64)
    y = np.zeros((N, 128, TK))
    for r in range(N):
        for j in range(N):
            y[r] += W2[j].T @ (silu(W1[j].T @ X[r]) * (W3[j].T @ X[r]))
    return {"y": y.astype(ml_dtypes.bfloat16)}

@@ -1,0 +1,172 @@
+from concourse.bass import DstId, RemoteDMATransfer
+from concourse.mybir import AluOpType, ActivationFunctionType
+
+P = 128
+WW = 3 * P
+GS = 4
+NGRP = 9
+GW = 3 * P
+
+SCRATCH = {
+    "xs": ("sbuf", [P, GS * P], "bfloat16"),
+    "ws": ("sbuf", [P, GS * WW], "bfloat16"),
+    "sil": ("sbuf", [P, NGRP * GW], "float32"),
+    "hh": ("sbuf", [P, NGRP * GW], "bfloat16"),
+    "pout": ("sbuf", [P, GS * P], "bfloat16"),
+    "pin": ("sbuf", [P, GS * P], "bfloat16"),
+    "yo": ("sbuf", [P, P], "bfloat16"),
+    "pa0": ("psum", [P, 512], "float32"), "pa1": ("psum", [P, 512], "float32"),
+    "pb0": ("psum", [P, 512], "float32"), "pb1": ("psum", [P, 512], "float32"),
+    "py0": ("psum", [P, 512], "float32"), "py1": ("psum", [P, 512], "float32"),
+    "py2": ("psum", [P, 512], "float32"), "py3": ("psum", [P, 512], "float32"),
+}
+SEMAPHORES = (["ldx", "ldw", "sent", "st", "rd0", "rd1", "rd2"]
+              + ["%s%d" % (n, i) for n in ("xa", "wa", "pr", "yb", "ev") for i in range(GS)]
+              + ["%s%d" % (n, i) for n in ("ga", "gb", "gs", "gh") for i in range(NGRP)])
+
+
+def _bits(mask):
+    return bin(mask).count("1")
+
+
+def _plan(c, cores, topo):
+    ch, di = topo.chip(c), topo.die(c)
+    wgrp = [k for k in cores if topo.chip(k) == ch or topo.mates(topo.chip(k), ch)]
+    xgrp = [k for k in cores if topo.die(k) == di and (topo.chip(k) == ch or topo.same_plane(topo.chip(k), ch))]
+    near = [k for k in wgrp if k != c and topo.chip(k) == ch]
+    far = sorted([k for k in wgrp if topo.chip(k) != ch], key=lambda k: topo.die(k) != di)
+    fmask = topo.mask(c, far[0])
+    for k in far:
+        fmask &= topo.mask(c, k)
+    nmask = topo.mask(c, near[0]) & ~fmask
+    xmask = fmask
+    for k in xgrp:
+        if k != c:
+            xmask &= topo.mask(c, k)
+    return {"wgrp": wgrp, "xgrp": xgrp, "near": near, "far": far, "fmask": fmask, "nmask": nmask, "xmask": xmask}
+
+
+def rank_program(g, core, T, topo):
+    if T.rank_of(core) is None:
+        return
+    sem = T.sem
+    pl = _plan(core, T.cores, topo)
+    wgrp, xgrp, near, far = pl["wgrp"], pl["xgrp"], pl["near"], pl["far"]
+    assert len(wgrp) == GS and len(xgrp) == GS and len(near) == 1 and len(far) == 2
+    wi, xi = wgrp.index(core), xgrp.index(core)
+    pe, act, dve = g.tensor, g.scalar, g.vector
+
+    def dst(c):
+        rid, pid, _ = topo.addr(c)
+        return DstId(rid=rid, pnc=pid)
+
+    def xcol(b):
+        return T.xs[:, b * P:(b + 1) * P]
+
+    def wcol(s, k):
+        return T.ws[:, s * WW + k * P:s * WW + (k + 1) * P]
+
+    g.sync.dma_start(xcol(xi), T.x[:]).then_inc(sem.ldx, 16)
+    g.scalar.dma_start(wcol(wi, 0), T.w1[:]).then_inc(sem.ldw, 16)
+    g.sync.dma_start(wcol(wi, 1), T.w3[:]).then_inc(sem.ldw, 16)
+    g.scalar.dma_start(wcol(wi, 2), T.w2[:]).then_inc(sem.ldw, 16)
+
+    def x_ready(b):
+        if b == xi:
+            return sem.ldx, 16
+        return sem["xa%d" % b], _bits(_plan(xgrp[b], T.cores, topo)["xmask"])
+
+    def w_ready(s):
+        if s == wi:
+            return sem.ldw, 48
+        q = _plan(wgrp[s], T.cores, topo)
+        return sem["wa%d" % s], _bits(q["nmask"] if core in q["near"] else q["fmask"])
+
+    sent = 0
+    xto = [xgrp[(xi + k) % GS] for k in range(1, GS)]
+    g.wait_ge(sem.ldx, 16)
+    g.remote_dma_fused([RemoteDMATransfer(dst_ids=[dst(c) for c in xto], dma_engine_mask=pl["xmask"],
+                                          remote_sem=sem["xa%d" % xi], srcs=[xcol(xi)],
+                                          dsts=[xcol(xi) for _ in xto])], local_sem=sem.sent)
+    sent += _bits(pl["xmask"])
+    wown = T.ws[:, wi * WW:(wi + 1) * WW]
+    g.wait_ge(sem.ldw, 48)
+    g.remote_dma_fused([RemoteDMATransfer(dst_ids=[dst(c) for c in far], dma_engine_mask=pl["fmask"],
+                                          remote_sem=sem["wa%d" % wi], srcs=[wown], dsts=[wown for _ in far]),
+                        RemoteDMATransfer(dst_ids=[dst(c) for c in near], dma_engine_mask=pl["nmask"],
+                                          remote_sem=sem["wa%d" % wi], srcs=[wown], dsts=[wown for _ in near])],
+                       local_sem=sem.sent)
+    sent += _bits(pl["fmask"]) + _bits(pl["nmask"])
+
+    rb = [(xi - k) % GS for k in range(1, GS)]
+    sn, f1, f2 = wgrp.index(near[0]), wgrp.index(far[0]), wgrp.index(far[1])
+    groups = ([[(wi, xi)], [(wi, b) for b in rb], [(sn, b) for b in rb]]
+              + [[(f1, b), (f2, b)] for b in rb] + [[(s, xi)] for s in (sn, f1, f2)])
+    assert len(groups) == NGRP
+    pa, pb = [T.pa0, T.pa1], [T.pb0, T.pb1]
+    py = [T.py0, T.py1, T.py2, T.py3]
+    ydone = {b: 0 for b in range(GS)}
+
+    def ab(gi):
+        if gi >= 2:
+            pe.wait_ge(sem["gs%d" % (gi - 2)], 1)
+            pe.wait_ge(sem["gh%d" % (gi - 2)], 1)
+        for k, (s, b) in enumerate(groups[gi]):
+            pe.wait_ge(*x_ready(b))
+            pe.wait_ge(*w_ready(s))
+            pe.matmul(pa[gi % 2][:, k * P:(k + 1) * P], wcol(s, 0), xcol(b), True, True).then_inc(sem["ga%d" % gi], 1)
+        for k, (s, b) in enumerate(groups[gi]):
+            pe.matmul(pb[gi % 2][:, k * P:(k + 1) * P], wcol(s, 1), xcol(b), True, True).then_inc(sem["gb%d" % gi], 1)
+
+    def yy(gi):
+        pe.wait_ge(sem["gh%d" % gi], 1)
+        for k, (s, b) in enumerate(groups[gi]):
+            pe.matmul(py[b][:, 0:P], wcol(s, 2), T.hh[:, gi * GW + k * P:gi * GW + (k + 1) * P],
+                      ydone[b] == 0, ydone[b] == GS - 1).then_inc(sem["yb%d" % b], 1)
+            ydone[b] += 1
+
+    ab(0), yy(0), ab(1), ab(2), yy(1), ab(3), yy(2), ab(4), yy(3), ab(5), yy(4), yy(5)
+    ab(6), ab(7), yy(6), ab(8), yy(7), yy(8)
+
+    for gi in range(NGRP):
+        n = len(groups[gi])
+        act.wait_ge(sem["ga%d" % gi], n)
+        act.activation(T.sil[:, gi * GW:gi * GW + n * P], pa[gi % 2][:, 0:n * P],
+                       ActivationFunctionType.Silu).then_inc(sem["gs%d" % gi], 1)
+
+    def hmul(gi):
+        n = len(groups[gi])
+        dve.wait_ge(sem["gs%d" % gi], 1)
+        dve.wait_ge(sem["gb%d" % gi], n)
+        dve.tensor_tensor(T.hh[:, gi * GW:gi * GW + n * P], T.sil[:, gi * GW:gi * GW + n * P],
+                          pb[gi % 2][:, 0:n * P], AluOpType.mult).then_inc(sem["gh%d" % gi], 1)
+
+    def evac(b):
+        dve.wait_ge(sem["yb%d" % b], GS)
+        dve.tensor_copy(T.pout[:, b * P:(b + 1) * P], py[b][:, 0:P]).then_inc(sem["ev%d" % b], 1)
+
+    for gi in range(5):
+        hmul(gi)
+    evac(rb[0]), hmul(5), evac(rb[1]), evac(rb[2]), hmul(6), hmul(7), hmul(8)
+
+    for b in rb:
+        rid, pid, _ = topo.addr(xgrp[b])
+        g.wait_ge(sem["ev%d" % b], 1)
+        g.remote_dma(T.pin[:, xi * P:(xi + 1) * P], T.pout[:, b * P:(b + 1) * P], sem["pr%d" % xi], sem.sent,
+                     pid, rid, pl["xmask"])
+        sent += _bits(pl["xmask"])
+
+    own = py[xi][:, 0:P]
+    dve.wait_ge(sem["yb%d" % xi], GS)
+    for k in range(1, GS):
+        j = (xi + k) % GS
+        dve.wait_ge(sem["pr%d" % j], _bits(_plan(xgrp[j], T.cores, topo)["xmask"]))
+        if k > 1:
+            dve.wait_ge(sem["rd%d" % (k - 2)], 1)
+        dve.tensor_tensor(T.yo[:] if k == GS - 1 else own, own, T.pin[:, j * P:(j + 1) * P],
+                          AluOpType.add).then_inc(sem["rd%d" % (k - 1)], 1)
+
+    g.sync.wait_ge(sem.rd2, 1)
+    g.sync.dma_start(T.y[:], T.yo[:]).then_inc(sem.st, 16)
+    g.sync.wait_ge(sem.st, 16)
+    g.wait_ge(sem.sent, sent)

@@ -4,8 +4,9 @@ from concourse.mybir import AluOpType, ActivationFunctionType
 P = 128
 WW = 3 * P
 GS = 4
-NGRP = 9
+NGRP = 8
 GW = 3 * P
+NPAIR = 3
 
 SCRATCH = {
     "xs": ("sbuf", [P, GS * P], "bfloat16"),
@@ -15,10 +16,9 @@ SCRATCH = {
     "pout": ("sbuf", [P, GS * P], "bfloat16"),
     "pin": ("sbuf", [P, GS * P], "bfloat16"),
     "yo": ("sbuf", [P, P], "bfloat16"),
-    "pa0": ("psum", [P, 512], "float32"), "pa1": ("psum", [P, 512], "float32"),
-    "pb0": ("psum", [P, 512], "float32"), "pb1": ("psum", [P, 512], "float32"),
+    "pa0": ("psum", [P, 512], "float32"), "pa1": ("psum", [P, 512], "float32"), "pa2": ("psum", [P, 512], "float32"),
+    "pb0": ("psum", [P, 512], "float32"), "pb1": ("psum", [P, 512], "float32"), "pb2": ("psum", [P, 512], "float32"),
     "py0": ("psum", [P, 512], "float32"), "py1": ("psum", [P, 512], "float32"),
-    "py2": ("psum", [P, 512], "float32"), "py3": ("psum", [P, 512], "float32"),
 }
 SEMAPHORES = (["ldx", "ldw", "sent", "st", "rd0", "rd1", "rd2"]
               + ["%s%d" % (n, i) for n in ("xa", "wa", "pr", "yb", "ev") for i in range(GS)]
@@ -101,37 +101,43 @@ def rank_program(g, core, T, topo):
     rb = [(xi - k) % GS for k in range(1, GS)]
     sn, f1, f2 = wgrp.index(near[0]), wgrp.index(far[0]), wgrp.index(far[1])
     groups = ([[(wi, xi)], [(wi, b) for b in rb], [(sn, b) for b in rb]]
-              + [[(f1, b), (f2, b)] for b in rb] + [[(s, xi)] for s in (sn, f1, f2)])
+              + [[(f1, b), (f2, b)] for b in rb] + [[(sn, xi), (f1, xi)], [(f2, xi)]])
     assert len(groups) == NGRP
-    pa, pb = [T.pa0, T.pa1], [T.pb0, T.pb1]
-    py = [T.py0, T.py1, T.py2, T.py3]
-    ydone = {b: 0 for b in range(GS)}
+    pa, pb = [T.pa0, T.pa1, T.pa2], [T.pb0, T.pb1, T.pb2]
+    ybank = {rb[0]: T.py0, rb[1]: T.py1, rb[2]: T.py0, xi: T.py1}
+    ybefore = {rb[0]: None, rb[1]: None, rb[2]: rb[0], xi: rb[1]}
 
     def ab(gi):
-        if gi >= 2:
-            pe.wait_ge(sem["gs%d" % (gi - 2)], 1)
-            pe.wait_ge(sem["gh%d" % (gi - 2)], 1)
+        if gi >= NPAIR:
+            pe.wait_ge(sem["gs%d" % (gi - NPAIR)], 1)
+            pe.wait_ge(sem["gh%d" % (gi - NPAIR)], 1)
         for k, (s, b) in enumerate(groups[gi]):
             pe.wait_ge(*x_ready(b))
             pe.wait_ge(*w_ready(s))
-            pe.matmul(pa[gi % 2][:, k * P:(k + 1) * P], wcol(s, 0), xcol(b), True, True).then_inc(sem["ga%d" % gi], 1)
+            pe.matmul(pa[gi % NPAIR][:, k * P:(k + 1) * P], wcol(s, 0), xcol(b), True,
+                      True).then_inc(sem["ga%d" % gi], 1)
         for k, (s, b) in enumerate(groups[gi]):
-            pe.matmul(pb[gi % 2][:, k * P:(k + 1) * P], wcol(s, 1), xcol(b), True, True).then_inc(sem["gb%d" % gi], 1)
+            pe.matmul(pb[gi % NPAIR][:, k * P:(k + 1) * P], wcol(s, 1), xcol(b), True,
+                      True).then_inc(sem["gb%d" % gi], 1)
 
-    def yy(gi):
-        pe.wait_ge(sem["gh%d" % gi], 1)
-        for k, (s, b) in enumerate(groups[gi]):
-            pe.matmul(py[b][:, 0:P], wcol(s, 2), T.hh[:, gi * GW + k * P:gi * GW + (k + 1) * P],
-                      ydone[b] == 0, ydone[b] == GS - 1).then_inc(sem["yb%d" % b], 1)
-            ydone[b] += 1
+    def ysum(b):
+        if ybefore[b] is not None:
+            pe.wait_ge(sem["ev%d" % ybefore[b]], 1)
+        units = [(gi, k, s) for gi in range(NGRP) for k, (s, bb) in enumerate(groups[gi]) if bb == b]
+        assert len(units) == GS
+        for i, (gi, k, s) in enumerate(units):
+            pe.wait_ge(sem["gh%d" % gi], 1)
+            pe.matmul(ybank[b][:, 0:P], wcol(s, 2), T.hh[:, gi * GW + k * P:gi * GW + (k + 1) * P],
+                      i == 0, i == GS - 1).then_inc(sem["yb%d" % b], 1)
 
-    ab(0), yy(0), ab(1), ab(2), yy(1), ab(3), yy(2), ab(4), yy(3), ab(5), yy(4), yy(5)
-    ab(6), ab(7), yy(6), ab(8), yy(7), yy(8)
+    for gi in range(6):
+        ab(gi)
+    ysum(rb[0]), ysum(rb[1]), ysum(rb[2]), ab(6), ab(7), ysum(xi)
 
     for gi in range(NGRP):
         n = len(groups[gi])
         act.wait_ge(sem["ga%d" % gi], n)
-        act.activation(T.sil[:, gi * GW:gi * GW + n * P], pa[gi % 2][:, 0:n * P],
+        act.activation(T.sil[:, gi * GW:gi * GW + n * P], pa[gi % NPAIR][:, 0:n * P],
                        ActivationFunctionType.Silu).then_inc(sem["gs%d" % gi], 1)
 
     def hmul(gi):
@@ -139,15 +145,15 @@ def rank_program(g, core, T, topo):
         dve.wait_ge(sem["gs%d" % gi], 1)
         dve.wait_ge(sem["gb%d" % gi], n)
         dve.tensor_tensor(T.hh[:, gi * GW:gi * GW + n * P], T.sil[:, gi * GW:gi * GW + n * P],
-                          pb[gi % 2][:, 0:n * P], AluOpType.mult).then_inc(sem["gh%d" % gi], 1)
+                          pb[gi % NPAIR][:, 0:n * P], AluOpType.mult).then_inc(sem["gh%d" % gi], 1)
 
     def evac(b):
         dve.wait_ge(sem["yb%d" % b], GS)
-        dve.tensor_copy(T.pout[:, b * P:(b + 1) * P], py[b][:, 0:P]).then_inc(sem["ev%d" % b], 1)
+        dve.tensor_copy(T.pout[:, b * P:(b + 1) * P], ybank[b][:, 0:P]).then_inc(sem["ev%d" % b], 1)
 
-    for gi in range(5):
+    for gi in range(6):
         hmul(gi)
-    evac(rb[0]), hmul(5), evac(rb[1]), evac(rb[2]), hmul(6), hmul(7), hmul(8)
+    evac(rb[0]), evac(rb[1]), evac(rb[2]), hmul(6), hmul(7)
 
     for b in rb:
         rid, pid, _ = topo.addr(xgrp[b])
@@ -156,7 +162,7 @@ def rank_program(g, core, T, topo):
                      pid, rid, pl["xmask"])
         sent += _bits(pl["xmask"])
 
-    own = py[xi][:, 0:P]
+    own = ybank[xi][:, 0:P]
     dve.wait_ge(sem["yb%d" % xi], GS)
     for k in range(1, GS):
         j = (xi + k) % GS

from concourse.bass import DstId, RemoteDMATransfer
from concourse.mybir import AluOpType, ActivationFunctionType

P = 128
WW = 3 * P
GS = 4
NGRP = 8
GW = 3 * P
NPAIR = 3

SCRATCH = {
    "xs": ("sbuf", [P, GS * P], "bfloat16"),
    "ws": ("sbuf", [P, GS * WW], "bfloat16"),
    "sil": ("sbuf", [P, NGRP * GW], "float32"),
    "hh": ("sbuf", [P, NGRP * GW], "bfloat16"),
    "pout": ("sbuf", [P, GS * P], "bfloat16"),
    "pin": ("sbuf", [P, GS * P], "bfloat16"),
    "yo": ("sbuf", [P, P], "bfloat16"),
    "pa0": ("psum", [P, 512], "float32"), "pa1": ("psum", [P, 512], "float32"), "pa2": ("psum", [P, 512], "float32"),
    "pb0": ("psum", [P, 512], "float32"), "pb1": ("psum", [P, 512], "float32"), "pb2": ("psum", [P, 512], "float32"),
    "py0": ("psum", [P, 512], "float32"), "py1": ("psum", [P, 512], "float32"),
}
SEMAPHORES = (["ldx", "ldw", "sent", "st", "rd0", "rd1", "rd2"]
              + ["%s%d" % (n, i) for n in ("xa", "wa", "pr", "yb", "ev") for i in range(GS)]
              + ["%s%d" % (n, i) for n in ("ga", "gb", "gs", "gh") for i in range(NGRP)])


def _bits(mask):
    return bin(mask).count("1")


def _plan(c, cores, topo):
    ch, di = topo.chip(c), topo.die(c)
    wgrp = [k for k in cores if topo.chip(k) == ch or topo.mates(topo.chip(k), ch)]
    xgrp = [k for k in cores if topo.die(k) == di and (topo.chip(k) == ch or topo.same_plane(topo.chip(k), ch))]
    near = [k for k in wgrp if k != c and topo.chip(k) == ch]
    far = sorted([k for k in wgrp if topo.chip(k) != ch], key=lambda k: topo.die(k) != di)
    fmask = topo.mask(c, far[0])
    for k in far:
        fmask &= topo.mask(c, k)
    nmask = topo.mask(c, near[0]) & ~fmask
    xmask = fmask
    for k in xgrp:
        if k != c:
            xmask &= topo.mask(c, k)
    return {"wgrp": wgrp, "xgrp": xgrp, "near": near, "far": far, "fmask": fmask, "nmask": nmask, "xmask": xmask}


def rank_program(g, core, T, topo):
    if T.rank_of(core) is None:
        return
    sem = T.sem
    pl = _plan(core, T.cores, topo)
    wgrp, xgrp, near, far = pl["wgrp"], pl["xgrp"], pl["near"], pl["far"]
    assert len(wgrp) == GS and len(xgrp) == GS and len(near) == 1 and len(far) == 2
    wi, xi = wgrp.index(core), xgrp.index(core)
    pe, act, dve = g.tensor, g.scalar, g.vector

    def dst(c):
        rid, pid, _ = topo.addr(c)
        return DstId(rid=rid, pnc=pid)

    def xcol(b):
        return T.xs[:, b * P:(b + 1) * P]

    def wcol(s, k):
        return T.ws[:, s * WW + k * P:s * WW + (k + 1) * P]

    g.sync.dma_start(xcol(xi), T.x[:]).then_inc(sem.ldx, 16)
    g.scalar.dma_start(wcol(wi, 0), T.w1[:]).then_inc(sem.ldw, 16)
    g.sync.dma_start(wcol(wi, 1), T.w3[:]).then_inc(sem.ldw, 16)
    g.scalar.dma_start(wcol(wi, 2), T.w2[:]).then_inc(sem.ldw, 16)

    def x_ready(b):
        if b == xi:
            return sem.ldx, 16
        return sem["xa%d" % b], _bits(_plan(xgrp[b], T.cores, topo)["xmask"])

    def w_ready(s):
        if s == wi:
            return sem.ldw, 48
        q = _plan(wgrp[s], T.cores, topo)
        return sem["wa%d" % s], _bits(q["nmask"] if core in q["near"] else q["fmask"])

    sent = 0
    xto = [xgrp[(xi + k) % GS] for k in range(1, GS)]
    g.wait_ge(sem.ldx, 16)
    g.remote_dma_fused([RemoteDMATransfer(dst_ids=[dst(c) for c in xto], dma_engine_mask=pl["xmask"],
                                          remote_sem=sem["xa%d" % xi], srcs=[xcol(xi)],
                                          dsts=[xcol(xi) for _ in xto])], local_sem=sem.sent)
    sent += _bits(pl["xmask"])
    wown = T.ws[:, wi * WW:(wi + 1) * WW]
    g.wait_ge(sem.ldw, 48)
    g.remote_dma_fused([RemoteDMATransfer(dst_ids=[dst(c) for c in far], dma_engine_mask=pl["fmask"],
                                          remote_sem=sem["wa%d" % wi], srcs=[wown], dsts=[wown for _ in far]),
                        RemoteDMATransfer(dst_ids=[dst(c) for c in near], dma_engine_mask=pl["nmask"],
                                          remote_sem=sem["wa%d" % wi], srcs=[wown], dsts=[wown for _ in near])],
                       local_sem=sem.sent)
    sent += _bits(pl["fmask"]) + _bits(pl["nmask"])

    rb = [(xi - k) % GS for k in range(1, GS)]
    sn, f1, f2 = wgrp.index(near[0]), wgrp.index(far[0]), wgrp.index(far[1])
    groups = ([[(wi, xi)], [(wi, b) for b in rb], [(sn, b) for b in rb]]
              + [[(f1, b), (f2, b)] for b in rb] + [[(sn, xi), (f1, xi)], [(f2, xi)]])
    assert len(groups) == NGRP
    pa, pb = [T.pa0, T.pa1, T.pa2], [T.pb0, T.pb1, T.pb2]
    ybank = {rb[0]: T.py0, rb[1]: T.py1, rb[2]: T.py0, xi: T.py1}
    ybefore = {rb[0]: None, rb[1]: None, rb[2]: rb[0], xi: rb[1]}

    def ab(gi):
        if gi >= NPAIR:
            pe.wait_ge(sem["gs%d" % (gi - NPAIR)], 1)
            pe.wait_ge(sem["gh%d" % (gi - NPAIR)], 1)
        for k, (s, b) in enumerate(groups[gi]):
            pe.wait_ge(*x_ready(b))
            pe.wait_ge(*w_ready(s))
            pe.matmul(pa[gi % NPAIR][:, k * P:(k + 1) * P], wcol(s, 0), xcol(b), True,
                      True).then_inc(sem["ga%d" % gi], 1)
        for k, (s, b) in enumerate(groups[gi]):
            pe.matmul(pb[gi % NPAIR][:, k * P:(k + 1) * P], wcol(s, 1), xcol(b), True,
                      True).then_inc(sem["gb%d" % gi], 1)

    def ysum(b):
        if ybefore[b] is not None:
            pe.wait_ge(sem["ev%d" % ybefore[b]], 1)
        units = [(gi, k, s) for gi in range(NGRP) for k, (s, bb) in enumerate(groups[gi]) if bb == b]
        assert len(units) == GS
        for i, (gi, k, s) in enumerate(units):
            pe.wait_ge(sem["gh%d" % gi], 1)
            pe.matmul(ybank[b][:, 0:P], wcol(s, 2), T.hh[:, gi * GW + k * P:gi * GW + (k + 1) * P],
                      i == 0, i == GS - 1).then_inc(sem["yb%d" % b], 1)

    for gi in range(6):
        ab(gi)
    ysum(rb[0]), ysum(rb[1]), ysum(rb[2]), ab(6), ab(7), ysum(xi)

    for gi in range(NGRP):
        n = len(groups[gi])
        act.wait_ge(sem["ga%d" % gi], n)
        act.activation(T.sil[:, gi * GW:gi * GW + n * P], pa[gi % NPAIR][:, 0:n * P],
                       ActivationFunctionType.Silu).then_inc(sem["gs%d" % gi], 1)

    def hmul(gi):
        n = len(groups[gi])
        dve.wait_ge(sem["gs%d" % gi], 1)
        dve.wait_ge(sem["gb%d" % gi], n)
        dve.tensor_tensor(T.hh[:, gi * GW:gi * GW + n * P], T.sil[:, gi * GW:gi * GW + n * P],
                          pb[gi % NPAIR][:, 0:n * P], AluOpType.mult).then_inc(sem["gh%d" % gi], 1)

    def evac(b):
        dve.wait_ge(sem["yb%d" % b], GS)
        dve.tensor_copy(T.pout[:, b * P:(b + 1) * P], ybank[b][:, 0:P]).then_inc(sem["ev%d" % b], 1)

    for gi in range(6):
        hmul(gi)
    evac(rb[0]), evac(rb[1]), evac(rb[2]), hmul(6), hmul(7)

    for b in rb:
        rid, pid, _ = topo.addr(xgrp[b])
        g.wait_ge(sem["ev%d" % b], 1)
        g.remote_dma(T.pin[:, xi * P:(xi + 1) * P], T.pout[:, b * P:(b + 1) * P], sem["pr%d" % xi], sem.sent,
                     pid, rid, pl["xmask"])
        sent += _bits(pl["xmask"])

    own = ybank[xi][:, 0:P]
    dve.wait_ge(sem["yb%d" % xi], GS)
    for k in range(1, GS):
        j = (xi + k) % GS
        dve.wait_ge(sem["pr%d" % j], _bits(_plan(xgrp[j], T.cores, topo)["xmask"]))
        if k > 1:
            dve.wait_ge(sem["rd%d" % (k - 2)], 1)
        dve.tensor_tensor(T.yo[:] if k == GS - 1 else own, own, T.pin[:, j * P:(j + 1) * P],
                          AluOpType.add).then_inc(sem["rd%d" % (k - 1)], 1)

    g.sync.wait_ge(sem.rd2, 1)
    g.sync.dma_start(T.y[:], T.yo[:]).then_inc(sem.st, 16)
    g.sync.wait_ge(sem.st, 16)
    g.wait_ge(sem.sent, sent)
